import numpy as np
import ml_dtypes


def mxq(x, axis, fmt="e4m3"):
    dtype, down = {"e4m3": (ml_dtypes.float8_e4m3fn, 7), "e5m2": (ml_dtypes.float8_e5m2, 14)}[fmt]
    v = np.moveaxis(np.asarray(x, np.float32).astype(ml_dtypes.bfloat16).astype(np.float64), axis, -1)
    blocks = v.reshape(v.shape[:-1] + (-1, 32))
    amax = np.abs(blocks).max(-1, keepdims=True)
    byte = np.maximum(np.where(amax > 0, np.frexp(amax)[1] - 1 + 127, 0) - down, 1)
    scale = np.exp2(byte - 127.0)
    codes = (blocks / scale).astype(np.float32).astype(dtype).astype(np.float64)
    return np.moveaxis((codes * scale).reshape(v.shape), -1, axis)


WIDE = False


def mx_kscale(k):
    if not WIDE:
        return np.ones(k)
    levels = np.array([10, -10, 5, -5, 0])
    if k % 512:
        return np.exp2(np.random.permutation(np.resize(levels, k // 32))).repeat(32)
    a = np.empty((k // 512, 16))
    for p in range(k // 512):
        a[p, :8] = np.random.permutation(np.resize(levels, 8))
        for g in range(8):
            far = levels[np.abs(levels - a[p, g]) >= 10]
            a[p, g + 8] = far[np.random.randint(len(far))]
    return np.exp2(a.ravel()).repeat(32)


def f64(x):
    return np.asarray(x).astype(np.float64)


def striped(idx):
    return np.tile(idx.reshape(-1, 16).T, (8, 1)).astype(np.uint16)


def unstriped(offs):
    return offs[:16].T.reshape(-1).astype(np.int64)


E2M1 = np.array([0.0, 0.5, 1.0, 1.5, 2.0, 3.0, 4.0, 6.0, -0.0, -0.5, -1.0, -1.5, -2.0, -3.0, -4.0, -6.0])


def pack_weight(w, fmt):
    k, n = w.shape
    w = f64(np.asarray(w, np.float32).astype(ml_dtypes.bfloat16)).reshape(k // 32, 32, n)
    amax = np.abs(w).max(1)
    if fmt == "e4m3":
        byte = np.frexp(amax)[1] - 1 + 127 - 7
    else:
        mant, ex = np.frexp(amax / 6.0)
        byte = np.where(mant > 0.5, ex, ex - 1) + 127
    byte = np.clip(np.where(amax > 0, byte, 1), 1, 254)
    scaled = (w * np.exp2(127.0 - byte)[:, None, :]).reshape(k, n).astype(np.float32)
    by_word = np.ascontiguousarray(scaled.reshape(k // 512, 128, 4, n).transpose(0, 1, 3, 2))
    if fmt == "e4m3":
        words = by_word.astype(ml_dtypes.float8_e4m3fn).view(np.uint8)
    else:
        c = by_word.astype(ml_dtypes.float4_e2m1fn).view(np.uint8) & 0xF
        words = (c[..., 0::2] | (c[..., 1::2] << 4)).reshape(k // 512, 128, 2 * n)
    return np.ascontiguousarray(words), np.ascontiguousarray(byte.astype(np.uint8).reshape(k // 512, 16, n))


def unpack_weight(words, scales, fmt):
    g, _, n = scales.shape
    words = np.ascontiguousarray(words).reshape(g, 128, n, -1)
    if fmt == "e4m3":
        vals = words.view(ml_dtypes.float8_e4m3fn).astype(np.float64)
    else:
        nib = np.empty((g, 128, n, 4), np.uint8)
        nib[..., 0::2] = words & 0xF
        nib[..., 1::2] = words >> 4
        vals = E2M1[nib]
    vals = vals * np.repeat(np.exp2(scales.astype(np.float64) - 127.0), 8, axis=1)[..., None]
    return vals.transpose(0, 1, 3, 2).reshape(g * 512, n)


def gelu(v):
    return 0.5 * v * (1.0 + np.tanh(np.sqrt(2.0 / np.pi) * (v + 0.044715 * v**3)))


K, H, T, S, T2, P = 1024, 512, 2048, 1024, 2048, 1024

def setup_inputs():
    n = np.random.standard_normal
    s = mx_kscale(K)[:, None]
    u = mx_kscale(H)[:, None]
    tab_words, tab_scales = pack_weight(n((K, T)) * s, "e4m3")
    w4_words, w4_scales = pack_weight(n((H, H)) / np.sqrt(H) / u * u.T, "e2m1")
    return {
        "tab_words": tab_words, "tab_scales": tab_scales,
        "offs": striped(np.random.permutation(T)[:S]),
        "w1": (n((K, H)) / np.sqrt(K) / s * u.T).astype(np.float32),
        "b1": (0.6 * n(H) * u[:, 0]).astype(np.float32),
        "page0": (n((H, T2)) * u).astype(np.float32),
        "wgs": np.exp(0.3 * n((128, S))).astype(np.float32),
        "offs2": striped(np.random.permutation(T2)[:S]),
        "offs3": striped(np.random.permutation(T2)[:P]),
        "base": (n((H, P)) * u).astype(np.float32),
        "w2": (n((H, H)) / np.sqrt(H) / u * u.T).astype(np.float32),
        "w4_words": w4_words, "w4_scales": w4_scales,
        "b2": (0.8 * n(H) * u[:, 0]).astype(np.float32),
        "wgo": np.exp(0.3 * n((128, P))).astype(np.float32),
        "offs4": striped(np.random.permutation(T2)[:P]),
    }

def reference(tab_words, tab_scales, offs, w1, b1, page0, wgs, offs2, offs3, base, w2, w4_words, w4_scales, b2, wgo, offs4):
    v = unpack_weight(tab_words, tab_scales, "e4m3")[:, unstriped(offs)]
    h = (mxq(f64(w1), 0, "e4m3").T @ v) + f64(b1)[:, None]
    page = f64(page0).copy()
    page[:, unstriped(offs2)] = np.tile(f64(wgs), (H // 128, 1)) * h
    x = page[:, unstriped(offs3)]
    d = x - f64(base)
    dq = mxq(d, 0, "e4m3")
    zq = mxq(np.abs(d), 0, "e4m3")
    w4 = unpack_weight(w4_words, w4_scales, "e2m1")
    e = mxq(f64(w2), 0, "e4m3").T @ dq + w4.T @ zq
    y = np.maximum(e + f64(b2)[:, None], x)
    page[:, unstriped(offs4)] = np.tile(f64(wgo), (H // 128, 1)) * y
    return page

@@ -1,0 +1,309 @@
+from contextlib import ExitStack
+
+import concourse.mybir as mybir
+from concourse.masks import make_identity
+
+K, H, T, S = 1024, 512, 2048, 1024
+FLOPS = 2 * K * H * S + 2 * 2 * H * H * S
+
+F32 = mybir.dt.float32
+BF16 = mybir.dt.bfloat16
+I32 = mybir.dt.int32
+U32 = mybir.dt.uint32
+U16 = mybir.dt.uint16
+U8 = mybir.dt.uint8
+FP8X4 = mybir.dt.float8_e4m3fn_x4
+FP4X4 = mybir.dt.float4_e2m1fn_x4
+ALU = mybir.AluOpType
+ACT = mybir.ActivationFunctionType
+
+P = 128
+PACK = 4
+PASSES = K // (P * PACK)
+TILES = H // P
+HALF = S // 2
+QUARTER = S // 4
+GROUP = 16
+
+
+def entries(offsets, first, count):
+    return offsets[:, first // GROUP : (first + count) // GROUP]
+
+
+def tile_list_chatter_map_rescore_kernel(
+    tc, tab_words, tab_scales, offs, w1, b1, page0, wgs, offs2, offs3, base, w2, w4_words, w4_scales, b2, wgo, offs4, out
+):
+    nc = tc.nc
+    with ExitStack() as ctx:
+        lists = ctx.enter_context(tc.tile_pool(name="lists", bufs=1))
+        sb = ctx.enter_context(tc.tile_pool(name="sb", bufs=1))
+        psum = ctx.enter_context(tc.psum_pool(name="psum", bufs=1))
+
+        def tile(shape, dtype, name, tag=None, bufs=1):
+            return sb.tile(shape, dtype, name=name, tag=tag or name, bufs=bufs, align_bytes=64)
+
+        def bank(name, tag, bufs):
+            return psum.tile([P, HALF], F32, name=name, tag=tag, bufs=bufs)
+
+        idx1 = lists.tile([P, S // GROUP], U16, name="idx1")
+        idx2 = lists.tile([P, S // GROUP], U16, name="idx2")
+        idx3 = lists.tile([P, S // GROUP], U16, name="idx3")
+        idx4 = lists.tile([P, S // GROUP], U16, name="idx4")
+
+        table_words = [tile([P, T], I32, f"table_words{a}") for a in range(PASSES)]
+        table_scales = tile([P, T], U8, "table_scales")
+        w1_raw = [tile([P, PASSES, PACK, P], F32, f"w1_raw{t}") for t in range(2)]
+        w1_raw_late = tile([P, PASSES, PACK, 2 * P], F32, "w1_raw_late")
+        page = [tile([P, T], F32, f"page{t}") for t in range(TILES)]
+        neg_base = [tile([P, S], F32, f"neg_base{t}") for t in range(TILES)]
+        wgs_sb = tile([P, S], F32, "wgs_sb", tag="wgs_then_x")
+        wgo_sb = tile([P, S], F32, "wgo_sb")
+        b1_sb = tile([P, TILES, 8], F32, "b1_sb")
+        b2_sb = tile([P, TILES, 8], F32, "b2_sb")
+        w2_raw = tile([P, PACK, H], F32, "w2_raw")
+        w4_codes = tile([P, 2 * H], U8, "w4_codes")
+        w4_plane = tile([P, H], U8, "w4_plane")
+        ident = tile([P, P], F32, "ident")
+
+        nc.gpsimd.memset(table_scales[:].bitcast(I32), 0)
+
+        def load_words(a):
+            nc.sync.dma_start(out=table_words[a][:], in_=tab_words[a].rearrange("p t i -> p (t i)").bitcast(I32))
+
+        def load_w1(dst, first, count):
+            for a in range(PASSES):
+                rows = w1[a * P * PACK : (a + 1) * P * PACK, first : first + count]
+                nc.sync.dma_start(out=dst[:, a, :, :], in_=rows.rearrange("(p i) c -> p i c", i=PACK))
+
+        def load_bias(dst, vec):
+            with nc.allow_non_contiguous_dma(reason="one bias value for each partition and row tile"):
+                nc.sync.dma_start(out=dst[:, :, 0], in_=vec.rearrange("(t p) -> p t", p=P))
+
+        def load_rows(dst, src, t):
+            nc.sync.dma_start(out=dst[t][:], in_=src[t * P : (t + 1) * P, :])
+
+        nc.sync.dma_start(idx1[:], offs)
+        nc.sync.dma_start(idx2[:], offs2)
+        nc.sync.dma_start(idx3[:], offs3)
+        nc.sync.dma_start(idx4[:], offs4)
+        load_bias(b1_sb, b1)
+        load_bias(b2_sb, b2)
+        load_words(0)
+        load_w1(w1_raw[0], 0, P)
+        nc.sync.dma_start(out=wgs_sb[:, :HALF], in_=wgs[:, :HALF])
+        for q in range(4):
+            nc.sync.dma_start(
+                out=table_scales[32 * q : 32 * q + 4 * PASSES, :].bitcast(I32),
+                in_=tab_scales[:, 4 * q : 4 * q + 4, :].bitcast(I32),
+            )
+        nc.gpsimd.memset(w4_plane[:].bitcast(I32), 0)
+        make_identity(nc, ident[:])
+        nc.sync.dma_start(out=w4_codes[:].bitcast(I32), in_=w4_words[0].bitcast(I32))
+        load_words(1)
+        load_rows(page, page0, 0)
+        load_w1(w1_raw[1], P, P)
+        load_w1(w1_raw_late, 2 * P, 2 * P)
+        nc.sync.dma_start(out=wgs_sb[:, HALF:], in_=wgs[:, HALF:])
+        load_rows(page, page0, 1)
+        load_rows(neg_base, base, 0)
+        load_rows(neg_base, base, 1)
+        load_rows(page, page0, 2)
+        nc.sync.dma_start(out=w2_raw[:], in_=w2.rearrange("(p i) c -> p i c", i=PACK))
+        for q in range(4):
+            nc.sync.dma_start(
+                out=w4_plane[32 * q : 32 * q + 4, :].bitcast(I32), in_=w4_scales[0, 4 * q : 4 * q + 4, :].bitcast(I32)
+            )
+        load_rows(neg_base, base, 2)
+        load_rows(neg_base, base, 3)
+        load_rows(page, page0, 3)
+        nc.sync.dma_start(out=wgo_sb[:], in_=wgo)
+
+        v_scales = [tile([P, HALF], U8, f"v_scales{h}") for h in range(2)]
+        v_words0 = tile([P, S], U32, "v_words0")
+        v_words1 = [tile([P, HALF], U32, f"v_words1_{h}") for h in range(2)]
+        w1_codes = [tile([P, PASSES * P], U32, f"w1_codes{t}") for t in range(TILES)]
+        w1_plane = [tile([P, PASSES * P], U8, f"w1_plane{t}") for t in range(TILES)]
+        h_sb = [tile([P, S], F32, f"h_sb{t}") for t in range(TILES)]
+
+        def quantize(codes, plane, grouped):
+            nc.vector.quantize_mx(out=codes.bitcast(FP8X4), scales=plane, in_=grouped)
+
+        def quantize_w1(t):
+            raw = w1_raw[t][:] if t < 2 else w1_raw_late[:, :, :, (t - 2) * P : (t - 1) * P]
+            grouped = tile([P, PASSES * P * PACK], BF16, f"w1_grouped{t}")
+            for a in range(PASSES):
+                nc.scalar.activation(
+                    out=grouped[:].rearrange("p (a c i) -> p a c i", a=PASSES, i=PACK)[:, a, :, :],
+                    in_=raw.rearrange("p a i c -> p a c i")[:, a, :, :],
+                    func=ACT.Copy,
+                )
+            quantize(w1_codes[t][:], w1_plane[t][:], grouped[:])
+
+        def make_h(t, half):
+            cols = slice(half * HALF, (half + 1) * HALF)
+            acc = bank(f"h_acc{t}_{half}", "acc", 4)
+            moving = [v_words0[:, cols], v_words1[half][:]]
+            for a in range(PASSES):
+                nc.tensor.matmul_mx(
+                    out=acc[:],
+                    lhsT=w1_codes[t][:, a * P : (a + 1) * P].bitcast(FP8X4),
+                    lhsT_scale=w1_plane[t][:, a * P : (a + 1) * P],
+                    rhs=moving[a].bitcast(FP8X4),
+                    rhs_scale=v_scales[half][4 * a :, :],
+                    start=(a == 0),
+                    stop=(a == PASSES - 1),
+                )
+            nc.scalar.activation(out=h_sb[t][:, cols], in_=acc[:], func=ACT.Identity, bias=b1_sb[:, t, 0:1])
+
+        def put(t, offsets, first, count, values, weights):
+            nc.vector.tensor_tensor(
+                page[t][:].indirect(entries(offsets, first, count)), values, weights[:, first : first + count], ALU.mult
+            )
+
+        def pick(t, first, count, dst):
+            nc.vector.tensor_copy(dst, page[t][:].indirect(entries(idx3, first, count)))
+
+        def departure_t(d_t, t, first, count, x):
+            blocks = count // P
+            acc = bank(f"dt_acc{t}_{first}", "dt_acc", 2)
+            for b in range(blocks):
+                dst = acc[:, b * P : (b + 1) * P]
+                nb = neg_base[t][:, first + b * P : first + (b + 1) * P]
+                nc.tensor.matmul(dst, nb, ident[:], start=True, stop=False, is_transpose=True)
+                nc.tensor.matmul(dst, x[:, b * P : (b + 1) * P], ident[:], start=False, stop=True, is_transpose=True)
+            b0 = (first % HALF) // P
+            nc.scalar.copy(
+                out=d_t[:].rearrange("j (b u q e) -> j b u q e", u=2, q=P, e=2)[:, b0 : b0 + blocks, :, 32 * t : 32 * t + 32, :],
+                in_=acc[:, :count].rearrange("j (b q u e) -> j b u q e", q=32, u=2, e=2),
+            )
+
+        def group_d_z(d_t, quarter, d_dst, z_dst):
+            words = d_t[:].bitcast(F32)
+            acc = bank(f"w_acc{quarter}", "w_acc", 2)
+            for u in range(2):
+                for bl in range(2):
+                    b = 2 * (quarter % 2) + bl
+                    src = words[:, (2 * b + u) * P : (2 * b + u + 1) * P]
+                    nc.tensor.transpose(acc[:, u * QUARTER + bl * P : u * QUARTER + (bl + 1) * P], src, ident[:])
+            nc.scalar.copy(
+                out=d_dst.bitcast(F32).rearrange("p (j u) -> p j u", u=2),
+                in_=acc[:].rearrange("p (u j) -> p j u", u=2),
+            )
+            nc.scalar.activation(
+                out=z_dst.rearrange("p (j u e) -> p j u e", u=2, e=2),
+                in_=acc[:].bitcast(BF16).rearrange("p (u j e) -> p j u e", u=2, e=2),
+                func=ACT.Abs,
+            )
+
+        nc.vector.tensor_copy(v_words0[:], table_words[0][:].bitcast(U32).indirect(idx1[:]))
+        quantize_w1(0)
+        for half in range(2):
+            window = table_words[1][:].bitcast(U32)
+            nc.vector.tensor_copy(v_scales[half][:], table_scales[:].indirect(entries(idx1, half * HALF, HALF)))
+            nc.vector.tensor_copy(v_words1[half][:], window.indirect(entries(idx1, half * HALF, HALF)))
+            make_h(0, half)
+        put(0, idx2, 0, HALF, h_sb[0][:, :HALF], wgs_sb)
+        for t in range(1, TILES):
+            quantize_w1(t)
+            make_h(t, 0)
+            make_h(t, 1)
+        put(0, idx2, HALF, HALF, h_sb[0][:, HALF:], wgs_sb)
+
+        for t in range(TILES):
+            nc.scalar.activation(out=neg_base[t][:], in_=neg_base[t][:], func=ACT.Copy, scale=-1.0)
+
+        w2_grouped = tile([P, H * PACK], BF16, "w2_grouped")
+        w2_codes = tile([P, H], U32, "w2_codes")
+        w2_plane = tile([P, H], U8, "w2_plane")
+        nc.scalar.activation(
+            out=w2_grouped[:].rearrange("p (c i) -> p c i", i=PACK), in_=w2_raw[:].rearrange("p i c -> p c i"), func=ACT.Copy
+        )
+        quantize(w2_codes[:], w2_plane[:], w2_grouped[:])
+
+        x0 = [tile([P, HALF], F32, f"x0_{t}") for t in range(TILES)]
+        d_t0 = tile([P, PACK * HALF], BF16, "d_t0", tag="d_t")
+        last = TILES - 1
+        for t in range(TILES):
+            if t > 0:
+                put(t, idx2, 0, S, h_sb[t][:], wgs_sb)
+            if t < last:
+                pick(t, 0, HALF, x0[t][:])
+                departure_t(d_t0, t, 0, HALF, x0[t])
+        for quarter in range(2):
+            cols = slice(quarter * QUARTER, (quarter + 1) * QUARTER)
+            pick(last, quarter * QUARTER, QUARTER, x0[last][:, cols])
+            departure_t(d_t0, last, quarter * QUARTER, QUARTER, x0[last][:, cols])
+
+        x1_early = tile([P, last, HALF], F32, "x1_early", tag="wgs_then_x")
+        for t in range(last):
+            pick(t, HALF, HALF, x1_early[:, t, :])
+
+        d_codes = [tile([P, HALF], U32, f"d_codes{h}") for h in range(2)]
+        d_plane = [tile([P, HALF], U8, f"d_plane{h}") for h in range(2)]
+        z_codes = [tile([P, HALF], U32, f"z_codes{h}") for h in range(2)]
+        z_plane = [tile([P, HALF], U8, f"z_plane{h}") for h in range(2)]
+        for quarter in range(2):
+            cols = slice(quarter * QUARTER, (quarter + 1) * QUARTER)
+            d_q = tile([P, PACK * QUARTER], BF16, f"d_q{quarter}")
+            z_q = tile([P, PACK * QUARTER], BF16, f"z_q{quarter}", tag=f"z_then_x{quarter}")
+            group_d_z(d_t0, quarter, d_q[:], z_q[:])
+            quantize(d_codes[0][:, cols], d_plane[0][:, cols], d_q[:])
+            quantize(z_codes[0][:, cols], z_plane[0][:, cols], z_q[:])
+
+        x1_last = tile([P, HALF], F32, "x1_last", tag="z_then_x1")
+        pick(last, HALF, HALF, x1_last[:])
+        x1 = [x1_early[:, t, :] for t in range(last)] + [x1_last[:]]
+
+        def score(t, half):
+            acc = bank(f"e_acc{t}_{half}", "acc", 4)
+            nc.tensor.matmul_mx(
+                out=acc[:],
+                lhsT=w2_codes[:, t * P : (t + 1) * P].bitcast(FP8X4),
+                lhsT_scale=w2_plane[:, t * P : (t + 1) * P],
+                rhs=d_codes[half][:].bitcast(FP8X4),
+                rhs_scale=d_plane[half][:],
+                start=True,
+                stop=False,
+            )
+            nc.tensor.matmul_mx(
+                out=acc[:],
+                lhsT=w4_codes[:, 2 * t * P : 2 * (t + 1) * P].bitcast(FP4X4),
+                lhsT_scale=w4_plane[:, t * P : (t + 1) * P],
+                rhs=z_codes[half][:].bitcast(FP8X4),
+                rhs_scale=z_plane[half][:],
+                start=False,
+                stop=True,
+            )
+            return acc
+
+        def larger(t, acc, x, y):
+            nc.vector.scalar_tensor_tensor(out=y, in0=acc[:], scalar=b2_sb[:, t, 0:1], in1=x, op0=ALU.add, op1=ALU.max)
+
+        acc0 = [score(t, 0) for t in range(TILES)]
+        y0 = [tile([P, HALF], F32, f"y0_{t}") for t in range(last)]
+        for t in range(last):
+            larger(t, acc0[t], x0[t][:], y0[t][:])
+        for t in range(last):
+            put(t, idx4, 0, HALF, y0[t][:], wgo_sb)
+
+        d_t1 = tile([P, PACK * HALF], BF16, "d_t1", tag="d_t")
+        for t in range(TILES):
+            departure_t(d_t1, t, HALF, HALF, x1[t])
+        d_h = tile([P, PACK * HALF], BF16, "d_h")
+        z_h = tile([P, PACK * HALF], BF16, "z_h", tag="z_then_y")
+        for quarter in range(2, 4):
+            cols = slice((quarter - 2) * PACK * QUARTER, (quarter - 1) * PACK * QUARTER)
+            group_d_z(d_t1, quarter, d_h[:, cols], z_h[:, cols])
+        quantize(d_codes[1][:], d_plane[1][:], d_h[:])
+        quantize(z_codes[1][:], z_plane[1][:], z_h[:])
+
+        y0_last = tile([P, HALF], F32, "y0_last", tag="z_then_y")
+        larger(last, acc0[last], x0[last][:], y0_last[:])
+        acc1 = [score(t, 1) for t in range(TILES)]
+        put(last, idx4, 0, HALF, y0_last[:], wgo_sb)
+        y1 = [tile([P, HALF], F32, f"y1_{t}") for t in range(TILES)]
+        for t in range(TILES):
+            larger(t, acc1[t], x1[t], y1[t][:])
+        for t in range(TILES):
+            put(t, idx4, HALF, HALF, y1[t][:], wgo_sb)
+            nc.sync.dma_start(out=out[t * P : (t + 1) * P, :], in_=page[t][:])

@@ -75,20 +75,18 @@ def tile_list_chatter_map_rescore_kernel(
                 rows = w1[a * P * PACK : (a + 1) * P * PACK, first : first + count]
                 nc.sync.dma_start(out=dst[:, a, :, :], in_=rows.rearrange("(p i) c -> p i c", i=PACK))
 
-        def load_bias(dst, vec):
+        def load_bias(queue, dst, vec):
             with nc.allow_non_contiguous_dma(reason="one bias value for each partition and row tile"):
-                nc.sync.dma_start(out=dst[:, :, 0], in_=vec.rearrange("(t p) -> p t", p=P))
+                queue.dma_start(out=dst[:, :, 0], in_=vec.rearrange("(t p) -> p t", p=P))
 
         def load_rows(dst, src, t):
             nc.sync.dma_start(out=dst[t][:], in_=src[t * P : (t + 1) * P, :])
 
+        load_words(0)
         nc.sync.dma_start(idx1[:], offs)
         nc.sync.dma_start(idx2[:], offs2)
         nc.sync.dma_start(idx3[:], offs3)
-        nc.sync.dma_start(idx4[:], offs4)
-        load_bias(b1_sb, b1)
-        load_bias(b2_sb, b2)
-        load_words(0)
+        load_words(1)
         load_w1(w1_raw[0], 0, P)
         nc.sync.dma_start(out=wgs_sb[:, :HALF], in_=wgs[:, :HALF])
         for q in range(4):
@@ -96,34 +94,35 @@ def tile_list_chatter_map_rescore_kernel(
                 out=table_scales[32 * q : 32 * q + 4 * PASSES, :].bitcast(I32),
                 in_=tab_scales[:, 4 * q : 4 * q + 4, :].bitcast(I32),
             )
+        load_bias(nc.gpsimd, b1_sb, b1)
         nc.gpsimd.memset(w4_plane[:].bitcast(I32), 0)
         make_identity(nc, ident[:])
-        nc.sync.dma_start(out=w4_codes[:].bitcast(I32), in_=w4_words[0].bitcast(I32))
-        load_words(1)
         load_rows(page, page0, 0)
         load_w1(w1_raw[1], P, P)
         load_w1(w1_raw_late, 2 * P, 2 * P)
         nc.sync.dma_start(out=wgs_sb[:, HALF:], in_=wgs[:, HALF:])
         load_rows(page, page0, 1)
-        load_rows(neg_base, base, 0)
-        load_rows(neg_base, base, 1)
-        load_rows(page, page0, 2)
         nc.sync.dma_start(out=w2_raw[:], in_=w2.rearrange("(p i) c -> p i c", i=PACK))
+        nc.sync.dma_start(out=w4_codes[:].bitcast(I32), in_=w4_words[0].bitcast(I32))
         for q in range(4):
             nc.sync.dma_start(
                 out=w4_plane[32 * q : 32 * q + 4, :].bitcast(I32), in_=w4_scales[0, 4 * q : 4 * q + 4, :].bitcast(I32)
             )
+        load_rows(neg_base, base, 0)
+        load_rows(neg_base, base, 1)
+        load_rows(page, page0, 2)
         load_rows(neg_base, base, 2)
         load_rows(neg_base, base, 3)
         load_rows(page, page0, 3)
+        load_bias(nc.sync, b2_sb, b2)
+        nc.sync.dma_start(idx4[:], offs4)
         nc.sync.dma_start(out=wgo_sb[:], in_=wgo)
 
-        v_scales = [tile([P, HALF], U8, f"v_scales{h}") for h in range(2)]
-        v_words0 = tile([P, S], U32, "v_words0")
-        v_words1 = [tile([P, HALF], U32, f"v_words1_{h}") for h in range(2)]
+        v_scales = tile([P, S], U8, "v_scales")
+        v_words = [tile([P, S], U32, f"v_words{a}") for a in range(PASSES)]
         w1_codes = [tile([P, PASSES * P], U32, f"w1_codes{t}") for t in range(TILES)]
         w1_plane = [tile([P, PASSES * P], U8, f"w1_plane{t}") for t in range(TILES)]
-        h_sb = [tile([P, S], F32, f"h_sb{t}") for t in range(TILES)]
+        h_sb = [tile([P, S], F32, f"h_sb{t}", tag=f"h_then_x{t}") for t in range(TILES)]
 
         def quantize(codes, plane, grouped):
             nc.vector.quantize_mx(out=codes.bitcast(FP8X4), scales=plane, in_=grouped)
@@ -139,21 +138,20 @@ def tile_list_chatter_map_rescore_kernel(
                 )
             quantize(w1_codes[t][:], w1_plane[t][:], grouped[:])
 
-        def make_h(t, half):
-            cols = slice(half * HALF, (half + 1) * HALF)
-            acc = bank(f"h_acc{t}_{half}", "acc", 4)
-            moving = [v_words0[:, cols], v_words1[half][:]]
+        def make_h(t, first, count):
+            cols = slice(first, first + count)
+            acc = bank(f"h_acc{t}_{first}", "acc", 4)[:, :count]
             for a in range(PASSES):
                 nc.tensor.matmul_mx(
-                    out=acc[:],
+                    out=acc,
                     lhsT=w1_codes[t][:, a * P : (a + 1) * P].bitcast(FP8X4),
                     lhsT_scale=w1_plane[t][:, a * P : (a + 1) * P],
-                    rhs=moving[a].bitcast(FP8X4),
-                    rhs_scale=v_scales[half][4 * a :, :],
+                    rhs=v_words[a][:, cols].bitcast(FP8X4),
+                    rhs_scale=v_scales[4 * a :, cols],
                     start=(a == 0),
                     stop=(a == PASSES - 1),
                 )
-            nc.scalar.activation(out=h_sb[t][:, cols], in_=acc[:], func=ACT.Identity, bias=b1_sb[:, t, 0:1])
+            nc.scalar.activation(out=h_sb[t][:, cols], in_=acc, func=ACT.Identity, bias=b1_sb[:, t, 0:1])
 
         def put(t, offsets, first, count, values, weights):
             nc.vector.tensor_tensor(
@@ -195,22 +193,20 @@ def tile_list_chatter_map_rescore_kernel(
                 func=ACT.Abs,
             )
 
-        nc.vector.tensor_copy(v_words0[:], table_words[0][:].bitcast(U32).indirect(idx1[:]))
+        for a in range(PASSES):
+            nc.vector.tensor_copy(v_words[a][:], table_words[a][:].bitcast(U32).indirect(idx1[:]))
         quantize_w1(0)
-        for half in range(2):
-            window = table_words[1][:].bitcast(U32)
-            nc.vector.tensor_copy(v_scales[half][:], table_scales[:].indirect(entries(idx1, half * HALF, HALF)))
-            nc.vector.tensor_copy(v_words1[half][:], window.indirect(entries(idx1, half * HALF, HALF)))
-            make_h(0, half)
-        put(0, idx2, 0, HALF, h_sb[0][:, :HALF], wgs_sb)
+        for first, count in ((0, QUARTER), (QUARTER, S - QUARTER)):
+            nc.vector.tensor_copy(v_scales[:, first : first + count], table_scales[:].indirect(entries(idx1, first, count)))
+        for first in (0, QUARTER):
+            make_h(0, first, QUARTER)
+            put(0, idx2, first, QUARTER, h_sb[0][:, first : first + QUARTER], wgs_sb)
+        make_h(0, HALF, HALF)
         for t in range(1, TILES):
             quantize_w1(t)
-            make_h(t, 0)
-            make_h(t, 1)
+            make_h(t, 0, HALF)
+            make_h(t, HALF, HALF)
         put(0, idx2, HALF, HALF, h_sb[0][:, HALF:], wgs_sb)
-
-        for t in range(TILES):
-            nc.scalar.activation(out=neg_base[t][:], in_=neg_base[t][:], func=ACT.Copy, scale=-1.0)
 
         w2_grouped = tile([P, H * PACK], BF16, "w2_grouped")
         w2_codes = tile([P, H], U32, "w2_codes")
@@ -220,15 +216,19 @@ def tile_list_chatter_map_rescore_kernel(
         )
         quantize(w2_codes[:], w2_plane[:], w2_grouped[:])
 
-        x0 = [tile([P, HALF], F32, f"x0_{t}") for t in range(TILES)]
+        for t in range(TILES):
+            nc.scalar.activation(out=neg_base[t][:], in_=neg_base[t][:], func=ACT.Copy, scale=-1.0)
+
+        x0 = []
         d_t0 = tile([P, PACK * HALF], BF16, "d_t0", tag="d_t")
         last = TILES - 1
-        for t in range(TILES):
-            if t > 0:
-                put(t, idx2, 0, S, h_sb[t][:], wgs_sb)
-            if t < last:
-                pick(t, 0, HALF, x0[t][:])
-                departure_t(d_t0, t, 0, HALF, x0[t])
+        for t in range(1, TILES):
+            put(t, idx2, 0, S, h_sb[t][:], wgs_sb)
+            for done in [t - 1, t] if t == last - 1 else [t - 1] if t < last else []:
+                x0.append(tile([P, HALF], F32, f"x0_{done}", tag=f"h_then_x{t}" if done < t else None))
+                pick(done, 0, HALF, x0[done][:])
+                departure_t(d_t0, done, 0, HALF, x0[done])
+        x0.append(tile([P, HALF], F32, f"x0_{last}"))
         for quarter in range(2):
             cols = slice(quarter * QUARTER, (quarter + 1) * QUARTER)
             pick(last, quarter * QUARTER, QUARTER, x0[last][:, cols])
@@ -250,41 +250,46 @@ def tile_list_chatter_map_rescore_kernel(
             quantize(d_codes[0][:, cols], d_plane[0][:, cols], d_q[:])
             quantize(z_codes[0][:, cols], z_plane[0][:, cols], z_q[:])
 
-        x1_last = tile([P, HALF], F32, "x1_last", tag="z_then_x1")
+        x1_last = tile([P, HALF], F32, "x1_last", tag="z_then_x0")
         pick(last, HALF, HALF, x1_last[:])
         x1 = [x1_early[:, t, :] for t in range(last)] + [x1_last[:]]
 
-        def score(t, half):
-            acc = bank(f"e_acc{t}_{half}", "acc", 4)
+        def score(t, first, count):
+            half = first // HALF
+            cols = slice(first % HALF, first % HALF + count)
+            acc = bank(f"e_acc{t}_{first}", "acc", 4)[:, :count]
             nc.tensor.matmul_mx(
-                out=acc[:],
+                out=acc,
                 lhsT=w2_codes[:, t * P : (t + 1) * P].bitcast(FP8X4),
                 lhsT_scale=w2_plane[:, t * P : (t + 1) * P],
-                rhs=d_codes[half][:].bitcast(FP8X4),
-                rhs_scale=d_plane[half][:],
+                rhs=d_codes[half][:, cols].bitcast(FP8X4),
+                rhs_scale=d_plane[half][:, cols],
                 start=True,
                 stop=False,
             )
             nc.tensor.matmul_mx(
-                out=acc[:],
+                out=acc,
                 lhsT=w4_codes[:, 2 * t * P : 2 * (t + 1) * P].bitcast(FP4X4),
                 lhsT_scale=w4_plane[:, t * P : (t + 1) * P],
-                rhs=z_codes[half][:].bitcast(FP8X4),
-                rhs_scale=z_plane[half][:],
+                rhs=z_codes[half][:, cols].bitcast(FP8X4),
+                rhs_scale=z_plane[half][:, cols],
                 start=False,
                 stop=True,
             )
             return acc
 
         def larger(t, acc, x, y):
-            nc.vector.scalar_tensor_tensor(out=y, in0=acc[:], scalar=b2_sb[:, t, 0:1], in1=x, op0=ALU.add, op1=ALU.max)
+            nc.vector.scalar_tensor_tensor(out=y, in0=acc, scalar=b2_sb[:, t, 0:1], in1=x, op0=ALU.add, op1=ALU.max)
 
-        acc0 = [score(t, 0) for t in range(TILES)]
-        y0 = [tile([P, HALF], F32, f"y0_{t}") for t in range(last)]
-        for t in range(last):
-            larger(t, acc0[t], x0[t][:], y0[t][:])
-        for t in range(last):
-            put(t, idx4, 0, HALF, y0[t][:], wgo_sb)
+        pieces = [(0, 0, QUARTER), (0, QUARTER, QUARTER)] + [(t, 0, HALF) for t in range(1, last)]
+        y0 = []
+        for t, first, count in pieces:
+            y = tile([P, count], F32, f"y0_{t}_{first}", tag="z_then_x1" if (t, first) == (0, 0) else None)
+            larger(t, score(t, first, count), x0[t][:, first : first + count], y[:])
+            y0.append(y)
+        acc0_last = score(last, 0, HALF)
+        for (t, first, count), y in zip(pieces, y0):
+            put(t, idx4, first, count, y[:], wgo_sb)
 
         d_t1 = tile([P, PACK * HALF], BF16, "d_t1", tag="d_t")
         for t in range(TILES):
@@ -298,8 +303,8 @@ def tile_list_chatter_map_rescore_kernel(
         quantize(z_codes[1][:], z_plane[1][:], z_h[:])
 
         y0_last = tile([P, HALF], F32, "y0_last", tag="z_then_y")
-        larger(last, acc0[last], x0[last][:], y0_last[:])
-        acc1 = [score(t, 1) for t in range(TILES)]
+        larger(last, acc0_last, x0[last][:], y0_last[:])
+        acc1 = [score(t, HALF, HALF) for t in range(TILES)]
         put(last, idx4, 0, HALF, y0_last[:], wgo_sb)
         y1 = [tile([P, HALF], F32, f"y1_{t}") for t in range(TILES)]
         for t in range(TILES):

@@ -60,6 +60,7 @@ def tile_list_chatter_map_rescore_kernel(
         wgo_sb = tile([P, S], F32, "wgo_sb")
         b1_sb = tile([P, TILES, 8], F32, "b1_sb")
         b2_sb = tile([P, TILES, 8], F32, "b2_sb")
+        turn = [psum.tile([P, HALF], F32, name=f"turn{i}") for i in range(2)]
         w2_raw = tile([P, PACK, H], F32, "w2_raw")
         w4_codes = tile([P, 2 * H], U8, "w4_codes")
         w4_plane = tile([P, H], U8, "w4_plane")
@@ -75,9 +76,9 @@ def tile_list_chatter_map_rescore_kernel(
                 rows = w1[a * P * PACK : (a + 1) * P * PACK, first : first + count]
                 nc.sync.dma_start(out=dst[:, a, :, :], in_=rows.rearrange("(p i) c -> p i c", i=PACK))
 
-        def load_bias(queue, dst, vec):
+        def load_bias(dst, vec, first, end):
             with nc.allow_non_contiguous_dma(reason="one bias value for each partition and row tile"):
-                queue.dma_start(out=dst[:, :, 0], in_=vec.rearrange("(t p) -> p t", p=P))
+                nc.sync.dma_start(out=dst[:, first:end, 0], in_=vec.rearrange("(t p) -> p t", p=P)[:, first:end])
 
         def load_rows(dst, src, t):
             nc.sync.dma_start(out=dst[t][:], in_=src[t * P : (t + 1) * P, :])
@@ -86,19 +87,20 @@ def tile_list_chatter_map_rescore_kernel(
         nc.sync.dma_start(idx1[:], offs)
         nc.sync.dma_start(idx2[:], offs2)
         nc.sync.dma_start(idx3[:], offs3)
+        load_bias(b1_sb, b1, 0, 1)
         load_words(1)
         load_w1(w1_raw[0], 0, P)
-        nc.sync.dma_start(out=wgs_sb[:, :HALF], in_=wgs[:, :HALF])
         for q in range(4):
             nc.sync.dma_start(
                 out=table_scales[32 * q : 32 * q + 4 * PASSES, :].bitcast(I32),
                 in_=tab_scales[:, 4 * q : 4 * q + 4, :].bitcast(I32),
             )
-        load_bias(nc.gpsimd, b1_sb, b1)
-        nc.gpsimd.memset(w4_plane[:].bitcast(I32), 0)
         make_identity(nc, ident[:])
+        nc.gpsimd.memset(w4_plane[:].bitcast(I32), 0)
         load_rows(page, page0, 0)
+        nc.sync.dma_start(out=wgs_sb[:, :HALF], in_=wgs[:, :HALF])
         load_w1(w1_raw[1], P, P)
+        load_bias(b1_sb, b1, 1, TILES)
         load_w1(w1_raw_late, 2 * P, 2 * P)
         nc.sync.dma_start(out=wgs_sb[:, HALF:], in_=wgs[:, HALF:])
         load_rows(page, page0, 1)
@@ -113,12 +115,12 @@ def tile_list_chatter_map_rescore_kernel(
         load_rows(page, page0, 2)
         load_rows(neg_base, base, 2)
         load_rows(neg_base, base, 3)
-        load_rows(page, page0, 3)
-        load_bias(nc.sync, b2_sb, b2)
+        load_bias(b2_sb, b2, 0, TILES)
         nc.sync.dma_start(idx4[:], offs4)
         nc.sync.dma_start(out=wgo_sb[:], in_=wgo)
+        load_rows(page, page0, 3)
 
-        v_scales = tile([P, S], U8, "v_scales")
+        v_scales_first = tile([P, QUARTER], U8, "v_scales_first")
         v_words = [tile([P, S], U32, f"v_words{a}") for a in range(PASSES)]
         w1_codes = [tile([P, PASSES * P], U32, f"w1_codes{t}") for t in range(TILES)]
         w1_plane = [tile([P, PASSES * P], U8, f"w1_plane{t}") for t in range(TILES)]
@@ -138,20 +140,25 @@ def tile_list_chatter_map_rescore_kernel(
                 )
             quantize(w1_codes[t][:], w1_plane[t][:], grouped[:])
 
-        def make_h(t, first, count):
-            cols = slice(first, first + count)
-            acc = bank(f"h_acc{t}_{first}", "acc", 4)[:, :count]
-            for a in range(PASSES):
-                nc.tensor.matmul_mx(
-                    out=acc,
-                    lhsT=w1_codes[t][:, a * P : (a + 1) * P].bitcast(FP8X4),
-                    lhsT_scale=w1_plane[t][:, a * P : (a + 1) * P],
-                    rhs=v_words[a][:, cols].bitcast(FP8X4),
-                    rhs_scale=v_scales[4 * a :, cols],
-                    start=(a == 0),
-                    stop=(a == PASSES - 1),
-                )
-            nc.scalar.activation(out=h_sb[t][:, cols], in_=acc, func=ACT.Identity, bias=b1_sb[:, t, 0:1])
+        def make_h(t, pieces):
+            acc = bank(f"h_acc{t}_{pieces[0][0]}", "acc", 6)
+            begin = pieces[0][0]
+            for first, count in pieces:
+                plane = v_scales_first if first < QUARTER else v_scales_rest[:, first - QUARTER : first - QUARTER + count]
+                for a in range(PASSES):
+                    nc.tensor.matmul_mx(
+                        out=acc[:, first - begin : first - begin + count],
+                        lhsT=w1_codes[t][:, a * P : (a + 1) * P].bitcast(FP8X4),
+                        lhsT_scale=w1_plane[t][:, a * P : (a + 1) * P],
+                        rhs=v_words[a][:, first : first + count].bitcast(FP8X4),
+                        rhs_scale=plane[4 * a :, :],
+                        start=(a == 0),
+                        stop=(a == PASSES - 1),
+                    )
+            total = sum(count for first, count in pieces)
+            nc.scalar.activation(
+                out=h_sb[t][:, begin : begin + total], in_=acc[:, :total], func=ACT.Identity, bias=b1_sb[:, t, 0:1]
+            )
 
         def put(t, offsets, first, count, values, weights):
             nc.vector.tensor_tensor(
@@ -161,9 +168,8 @@ def tile_list_chatter_map_rescore_kernel(
         def pick(t, first, count, dst):
             nc.vector.tensor_copy(dst, page[t][:].indirect(entries(idx3, first, count)))
 
-        def departure_t(d_t, t, first, count, x):
+        def departure_t(acc, d_t, t, first, count, x):
             blocks = count // P
-            acc = bank(f"dt_acc{t}_{first}", "dt_acc", 2)
             for b in range(blocks):
                 dst = acc[:, b * P : (b + 1) * P]
                 nb = neg_base[t][:, first + b * P : first + (b + 1) * P]
@@ -177,7 +183,7 @@ def tile_list_chatter_map_rescore_kernel(
 
         def group_d_z(d_t, quarter, d_dst, z_dst):
             words = d_t[:].bitcast(F32)
-            acc = bank(f"w_acc{quarter}", "w_acc", 2)
+            acc = turn[quarter % 2]
             for u in range(2):
                 for bl in range(2):
                     b = 2 * (quarter % 2) + bl
@@ -187,25 +193,22 @@ def tile_list_chatter_map_rescore_kernel(
                 out=d_dst.bitcast(F32).rearrange("p (j u) -> p j u", u=2),
                 in_=acc[:].rearrange("p (u j) -> p j u", u=2),
             )
-            nc.scalar.activation(
-                out=z_dst.rearrange("p (j u e) -> p j u e", u=2, e=2),
-                in_=acc[:].bitcast(BF16).rearrange("p (u j e) -> p j u e", u=2, e=2),
-                func=ACT.Abs,
-            )
+            nc.scalar.activation(out=z_dst, in_=d_dst, func=ACT.Abs)
 
         for a in range(PASSES):
             nc.vector.tensor_copy(v_words[a][:], table_words[a][:].bitcast(U32).indirect(idx1[:]))
         quantize_w1(0)
-        for first, count in ((0, QUARTER), (QUARTER, S - QUARTER)):
-            nc.vector.tensor_copy(v_scales[:, first : first + count], table_scales[:].indirect(entries(idx1, first, count)))
+        v_scales_rest = tile([P, S - QUARTER], U8, "v_scales_rest", tag="w1_grouped0")
+        nc.vector.tensor_copy(v_scales_first[:], table_scales[:].indirect(entries(idx1, 0, QUARTER)))
+        nc.vector.tensor_copy(v_scales_rest[:], table_scales[:].indirect(entries(idx1, QUARTER, S - QUARTER)))
         for first in (0, QUARTER):
-            make_h(0, first, QUARTER)
+            make_h(0, [(first, QUARTER)])
             put(0, idx2, first, QUARTER, h_sb[0][:, first : first + QUARTER], wgs_sb)
-        make_h(0, HALF, HALF)
+        make_h(0, [(HALF, HALF)])
         for t in range(1, TILES):
             quantize_w1(t)
-            make_h(t, 0, HALF)
-            make_h(t, HALF, HALF)
+            make_h(t, [(0, QUARTER), (QUARTER, QUARTER)])
+            make_h(t, [(HALF, HALF)])
         put(0, idx2, HALF, HALF, h_sb[0][:, HALF:], wgs_sb)
 
         w2_grouped = tile([P, H * PACK], BF16, "w2_grouped")
@@ -227,12 +230,12 @@ def tile_list_chatter_map_rescore_kernel(
             for done in [t - 1, t] if t == last - 1 else [t - 1] if t < last else []:
                 x0.append(tile([P, HALF], F32, f"x0_{done}", tag=f"h_then_x{t}" if done < t else None))
                 pick(done, 0, HALF, x0[done][:])
-                departure_t(d_t0, done, 0, HALF, x0[done])
+                departure_t(turn[(done + 1) % 2], d_t0, done, 0, HALF, x0[done])
         x0.append(tile([P, HALF], F32, f"x0_{last}"))
         for quarter in range(2):
             cols = slice(quarter * QUARTER, (quarter + 1) * QUARTER)
             pick(last, quarter * QUARTER, QUARTER, x0[last][:, cols])
-            departure_t(d_t0, last, quarter * QUARTER, QUARTER, x0[last][:, cols])
+            departure_t(turn[quarter], d_t0, last, quarter * QUARTER, QUARTER, x0[last][:, cols])
 
         x1_early = tile([P, last, HALF], F32, "x1_early", tag="wgs_then_x")
         for t in range(last):
@@ -257,7 +260,7 @@ def tile_list_chatter_map_rescore_kernel(
         def score(t, first, count):
             half = first // HALF
             cols = slice(first % HALF, first % HALF + count)
-            acc = bank(f"e_acc{t}_{first}", "acc", 4)[:, :count]
+            acc = bank(f"e_acc{t}_{first}", "acc", 6)[:, :count]
             nc.tensor.matmul_mx(
                 out=acc,
                 lhsT=w2_codes[:, t * P : (t + 1) * P].bitcast(FP8X4),
@@ -281,19 +284,20 @@ def tile_list_chatter_map_rescore_kernel(
         def larger(t, acc, x, y):
             nc.vector.scalar_tensor_tensor(out=y, in0=acc, scalar=b2_sb[:, t, 0:1], in1=x, op0=ALU.add, op1=ALU.max)
 
-        pieces = [(0, 0, QUARTER), (0, QUARTER, QUARTER)] + [(t, 0, HALF) for t in range(1, last)]
+        pieces = [(0, 0, QUARTER), (0, QUARTER, QUARTER), (1, 0, HALF)]
         y0 = []
         for t, first, count in pieces:
             y = tile([P, count], F32, f"y0_{t}_{first}", tag="z_then_x1" if (t, first) == (0, 0) else None)
             larger(t, score(t, first, count), x0[t][:, first : first + count], y[:])
             y0.append(y)
-        acc0_last = score(last, 0, HALF)
         for (t, first, count), y in zip(pieces, y0):
             put(t, idx4, first, count, y[:], wgo_sb)
 
         d_t1 = tile([P, PACK * HALF], BF16, "d_t1", tag="d_t")
         for t in range(TILES):
-            departure_t(d_t1, t, HALF, HALF, x1[t])
+            departure_t(turn[t % 2], d_t1, t, HALF, HALF, x1[t])
+        held = range(2, TILES)
+        acc0_held = {t: score(t, 0, HALF) for t in held}
         d_h = tile([P, PACK * HALF], BF16, "d_h")
         z_h = tile([P, PACK * HALF], BF16, "z_h", tag="z_then_y")
         for quarter in range(2, 4):
@@ -302,10 +306,12 @@ def tile_list_chatter_map_rescore_kernel(
         quantize(d_codes[1][:], d_plane[1][:], d_h[:])
         quantize(z_codes[1][:], z_plane[1][:], z_h[:])
 
-        y0_last = tile([P, HALF], F32, "y0_last", tag="z_then_y")
-        larger(last, acc0_last, x0[last][:], y0_last[:])
+        y0_held = tile([P, len(held) * HALF], F32, "y0_held", tag="z_then_y")
+        for i, t in enumerate(held):
+            larger(t, acc0_held[t], x0[t][:], y0_held[:, i * HALF : (i + 1) * HALF])
         acc1 = [score(t, HALF, HALF) for t in range(TILES)]
-        put(last, idx4, 0, HALF, y0_last[:], wgo_sb)
+        for i, t in enumerate(held):
+            put(t, idx4, 0, HALF, y0_held[:, i * HALF : (i + 1) * HALF], wgo_sb)
         y1 = [tile([P, HALF], F32, f"y1_{t}") for t in range(TILES)]
         for t in range(TILES):
             larger(t, acc1[t], x1[t], y1[t][:])

@@ -52,8 +52,7 @@ def tile_list_chatter_map_rescore_kernel(
 
         table_words = [tile([P, T], I32, f"table_words{a}") for a in range(PASSES)]
         table_scales = tile([P, T], U8, "table_scales")
-        w1_raw = [tile([P, PASSES, PACK, P], F32, f"w1_raw{t}") for t in range(2)]
-        w1_raw_late = tile([P, PASSES, PACK, 2 * P], F32, "w1_raw_late")
+        w1_raw = [tile([P, PASSES, PACK, 2 * P], F32, f"w1_raw{pair}") for pair in range(2)]
         page = [tile([P, T], F32, f"page{t}") for t in range(TILES)]
         neg_base = [tile([P, S], F32, f"neg_base{t}") for t in range(TILES)]
         wgs_sb = tile([P, S], F32, "wgs_sb", tag="wgs_then_x")
@@ -89,7 +88,7 @@ def tile_list_chatter_map_rescore_kernel(
         nc.sync.dma_start(idx3[:], offs3)
         load_bias(b1_sb, b1, 0, 1)
         load_words(1)
-        load_w1(w1_raw[0], 0, P)
+        load_w1(w1_raw[0], 0, 2 * P)
         for q in range(4):
             nc.sync.dma_start(
                 out=table_scales[32 * q : 32 * q + 4 * PASSES, :].bitcast(I32),
@@ -98,11 +97,10 @@ def tile_list_chatter_map_rescore_kernel(
         make_identity(nc, ident[:])
         nc.gpsimd.memset(w4_plane[:].bitcast(I32), 0)
         load_rows(page, page0, 0)
-        nc.sync.dma_start(out=wgs_sb[:, :HALF], in_=wgs[:, :HALF])
-        load_w1(w1_raw[1], P, P)
+        nc.sync.dma_start(out=wgs_sb[:, :QUARTER], in_=wgs[:, :QUARTER])
+        nc.sync.dma_start(out=wgs_sb[:, QUARTER:], in_=wgs[:, QUARTER:])
         load_bias(b1_sb, b1, 1, TILES)
-        load_w1(w1_raw_late, 2 * P, 2 * P)
-        nc.sync.dma_start(out=wgs_sb[:, HALF:], in_=wgs[:, HALF:])
+        load_w1(w1_raw[1], 2 * P, 2 * P)
         load_rows(page, page0, 1)
         nc.sync.dma_start(out=w2_raw[:], in_=w2.rearrange("(p i) c -> p i c", i=PACK))
         nc.sync.dma_start(out=w4_codes[:].bitcast(I32), in_=w4_words[0].bitcast(I32))
@@ -130,7 +128,7 @@ def tile_list_chatter_map_rescore_kernel(
             nc.vector.quantize_mx(out=codes.bitcast(FP8X4), scales=plane, in_=grouped)
 
         def quantize_w1(t):
-            raw = w1_raw[t][:] if t < 2 else w1_raw_late[:, :, :, (t - 2) * P : (t - 1) * P]
+            raw = w1_raw[t // 2][:, :, :, (t % 2) * P : (t % 2 + 1) * P]
             grouped = tile([P, PASSES * P * PACK], BF16, f"w1_grouped{t}")
             for a in range(PASSES):
                 nc.scalar.activation(

from contextlib import ExitStack

import concourse.mybir as mybir
from concourse.masks import make_identity

K, H, T, S = 1024, 512, 2048, 1024
FLOPS = 2 * K * H * S + 2 * 2 * H * H * S

F32 = mybir.dt.float32
BF16 = mybir.dt.bfloat16
I32 = mybir.dt.int32
U32 = mybir.dt.uint32
U16 = mybir.dt.uint16
U8 = mybir.dt.uint8
FP8X4 = mybir.dt.float8_e4m3fn_x4
FP4X4 = mybir.dt.float4_e2m1fn_x4
ALU = mybir.AluOpType
ACT = mybir.ActivationFunctionType

P = 128
PACK = 4
PASSES = K // (P * PACK)
TILES = H // P
HALF = S // 2
QUARTER = S // 4
GROUP = 16


def entries(offsets, first, count):
    return offsets[:, first // GROUP : (first + count) // GROUP]


def tile_list_chatter_map_rescore_kernel(
    tc, tab_words, tab_scales, offs, w1, b1, page0, wgs, offs2, offs3, base, w2, w4_words, w4_scales, b2, wgo, offs4, out
):
    nc = tc.nc
    with ExitStack() as ctx:
        lists = ctx.enter_context(tc.tile_pool(name="lists", bufs=1))
        sb = ctx.enter_context(tc.tile_pool(name="sb", bufs=1))
        psum = ctx.enter_context(tc.psum_pool(name="psum", bufs=1))

        def tile(shape, dtype, name, tag=None, bufs=1):
            return sb.tile(shape, dtype, name=name, tag=tag or name, bufs=bufs, align_bytes=64)

        def bank(name, tag, bufs):
            return psum.tile([P, HALF], F32, name=name, tag=tag, bufs=bufs)

        idx1 = lists.tile([P, S // GROUP], U16, name="idx1")
        idx2 = lists.tile([P, S // GROUP], U16, name="idx2")
        idx3 = lists.tile([P, S // GROUP], U16, name="idx3")
        idx4 = lists.tile([P, S // GROUP], U16, name="idx4")

        table_words = [tile([P, T], I32, f"table_words{a}") for a in range(PASSES)]
        table_scales = tile([P, T], U8, "table_scales")
        w1_raw = [tile([P, PASSES, PACK, 2 * P], F32, f"w1_raw{pair}") for pair in range(2)]
        page = [tile([P, T], F32, f"page{t}") for t in range(TILES)]
        neg_base = [tile([P, S], F32, f"neg_base{t}") for t in range(TILES)]
        wgs_sb = tile([P, S], F32, "wgs_sb", tag="wgs_then_x")
        wgo_sb = tile([P, S], F32, "wgo_sb")
        b1_sb = tile([P, TILES, 8], F32, "b1_sb")
        b2_sb = tile([P, TILES, 8], F32, "b2_sb")
        turn = [psum.tile([P, HALF], F32, name=f"turn{i}") for i in range(2)]
        w2_raw = tile([P, PACK, H], F32, "w2_raw")
        w4_codes = tile([P, 2 * H], U8, "w4_codes")
        w4_plane = tile([P, H], U8, "w4_plane")
        ident = tile([P, P], F32, "ident")

        nc.gpsimd.memset(table_scales[:].bitcast(I32), 0)

        def load_words(a):
            nc.sync.dma_start(out=table_words[a][:], in_=tab_words[a].rearrange("p t i -> p (t i)").bitcast(I32))

        def load_w1(dst, first, count):
            for a in range(PASSES):
                rows = w1[a * P * PACK : (a + 1) * P * PACK, first : first + count]
                nc.sync.dma_start(out=dst[:, a, :, :], in_=rows.rearrange("(p i) c -> p i c", i=PACK))

        def load_bias(dst, vec, first, end):
            with nc.allow_non_contiguous_dma(reason="one bias value for each partition and row tile"):
                nc.sync.dma_start(out=dst[:, first:end, 0], in_=vec.rearrange("(t p) -> p t", p=P)[:, first:end])

        def load_rows(dst, src, t):
            nc.sync.dma_start(out=dst[t][:], in_=src[t * P : (t + 1) * P, :])

        load_words(0)
        nc.sync.dma_start(idx1[:], offs)
        nc.sync.dma_start(idx2[:], offs2)
        nc.sync.dma_start(idx3[:], offs3)
        load_bias(b1_sb, b1, 0, 1)
        load_words(1)
        load_w1(w1_raw[0], 0, 2 * P)
        for q in range(4):
            nc.sync.dma_start(
                out=table_scales[32 * q : 32 * q + 4 * PASSES, :].bitcast(I32),
                in_=tab_scales[:, 4 * q : 4 * q + 4, :].bitcast(I32),
            )
        make_identity(nc, ident[:])
        nc.gpsimd.memset(w4_plane[:].bitcast(I32), 0)
        load_rows(page, page0, 0)
        nc.sync.dma_start(out=wgs_sb[:, :QUARTER], in_=wgs[:, :QUARTER])
        nc.sync.dma_start(out=wgs_sb[:, QUARTER:], in_=wgs[:, QUARTER:])
        load_bias(b1_sb, b1, 1, TILES)
        load_w1(w1_raw[1], 2 * P, 2 * P)
        load_rows(page, page0, 1)
        nc.sync.dma_start(out=w2_raw[:], in_=w2.rearrange("(p i) c -> p i c", i=PACK))
        nc.sync.dma_start(out=w4_codes[:].bitcast(I32), in_=w4_words[0].bitcast(I32))
        for q in range(4):
            nc.sync.dma_start(
                out=w4_plane[32 * q : 32 * q + 4, :].bitcast(I32), in_=w4_scales[0, 4 * q : 4 * q + 4, :].bitcast(I32)
            )
        load_rows(neg_base, base, 0)
        load_rows(neg_base, base, 1)
        load_rows(page, page0, 2)
        load_rows(neg_base, base, 2)
        load_rows(neg_base, base, 3)
        load_bias(b2_sb, b2, 0, TILES)
        nc.sync.dma_start(idx4[:], offs4)
        nc.sync.dma_start(out=wgo_sb[:], in_=wgo)
        load_rows(page, page0, 3)

        v_scales_first = tile([P, QUARTER], U8, "v_scales_first")
        v_words = [tile([P, S], U32, f"v_words{a}") for a in range(PASSES)]
        w1_codes = [tile([P, PASSES * P], U32, f"w1_codes{t}") for t in range(TILES)]
        w1_plane = [tile([P, PASSES * P], U8, f"w1_plane{t}") for t in range(TILES)]
        h_sb = [tile([P, S], F32, f"h_sb{t}", tag=f"h_then_x{t}") for t in range(TILES)]

        def quantize(codes, plane, grouped):
            nc.vector.quantize_mx(out=codes.bitcast(FP8X4), scales=plane, in_=grouped)

        def quantize_w1(t):
            raw = w1_raw[t // 2][:, :, :, (t % 2) * P : (t % 2 + 1) * P]
            grouped = tile([P, PASSES * P * PACK], BF16, f"w1_grouped{t}")
            for a in range(PASSES):
                nc.scalar.activation(
                    out=grouped[:].rearrange("p (a c i) -> p a c i", a=PASSES, i=PACK)[:, a, :, :],
                    in_=raw.rearrange("p a i c -> p a c i")[:, a, :, :],
                    func=ACT.Copy,
                )
            quantize(w1_codes[t][:], w1_plane[t][:], grouped[:])

        def make_h(t, pieces):
            acc = bank(f"h_acc{t}_{pieces[0][0]}", "acc", 6)
            begin = pieces[0][0]
            for first, count in pieces:
                plane = v_scales_first if first < QUARTER else v_scales_rest[:, first - QUARTER : first - QUARTER + count]
                for a in range(PASSES):
                    nc.tensor.matmul_mx(
                        out=acc[:, first - begin : first - begin + count],
                        lhsT=w1_codes[t][:, a * P : (a + 1) * P].bitcast(FP8X4),
                        lhsT_scale=w1_plane[t][:, a * P : (a + 1) * P],
                        rhs=v_words[a][:, first : first + count].bitcast(FP8X4),
                        rhs_scale=plane[4 * a :, :],
                        start=(a == 0),
                        stop=(a == PASSES - 1),
                    )
            total = sum(count for first, count in pieces)
            nc.scalar.activation(
                out=h_sb[t][:, begin : begin + total], in_=acc[:, :total], func=ACT.Identity, bias=b1_sb[:, t, 0:1]
            )

        def put(t, offsets, first, count, values, weights):
            nc.vector.tensor_tensor(
                page[t][:].indirect(entries(offsets, first, count)), values, weights[:, first : first + count], ALU.mult
            )

        def pick(t, first, count, dst):
            nc.vector.tensor_copy(dst, page[t][:].indirect(entries(idx3, first, count)))

        def departure_t(acc, d_t, t, first, count, x):
            blocks = count // P
            for b in range(blocks):
                dst = acc[:, b * P : (b + 1) * P]
                nb = neg_base[t][:, first + b * P : first + (b + 1) * P]
                nc.tensor.matmul(dst, nb, ident[:], start=True, stop=False, is_transpose=True)
                nc.tensor.matmul(dst, x[:, b * P : (b + 1) * P], ident[:], start=False, stop=True, is_transpose=True)
            b0 = (first % HALF) // P
            nc.scalar.copy(
                out=d_t[:].rearrange("j (b u q e) -> j b u q e", u=2, q=P, e=2)[:, b0 : b0 + blocks, :, 32 * t : 32 * t + 32, :],
                in_=acc[:, :count].rearrange("j (b q u e) -> j b u q e", q=32, u=2, e=2),
            )

        def group_d_z(d_t, quarter, d_dst, z_dst):
            words = d_t[:].bitcast(F32)
            acc = turn[quarter % 2]
            for u in range(2):
                for bl in range(2):
                    b = 2 * (quarter % 2) + bl
                    src = words[:, (2 * b + u) * P : (2 * b + u + 1) * P]
                    nc.tensor.transpose(acc[:, u * QUARTER + bl * P : u * QUARTER + (bl + 1) * P], src, ident[:])
            nc.scalar.copy(
                out=d_dst.bitcast(F32).rearrange("p (j u) -> p j u", u=2),
                in_=acc[:].rearrange("p (u j) -> p j u", u=2),
            )
            nc.scalar.activation(out=z_dst, in_=d_dst, func=ACT.Abs)

        for a in range(PASSES):
            nc.vector.tensor_copy(v_words[a][:], table_words[a][:].bitcast(U32).indirect(idx1[:]))
        quantize_w1(0)
        v_scales_rest = tile([P, S - QUARTER], U8, "v_scales_rest", tag="w1_grouped0")
        nc.vector.tensor_copy(v_scales_first[:], table_scales[:].indirect(entries(idx1, 0, QUARTER)))
        nc.vector.tensor_copy(v_scales_rest[:], table_scales[:].indirect(entries(idx1, QUARTER, S - QUARTER)))
        for first in (0, QUARTER):
            make_h(0, [(first, QUARTER)])
            put(0, idx2, first, QUARTER, h_sb[0][:, first : first + QUARTER], wgs_sb)
        make_h(0, [(HALF, HALF)])
        for t in range(1, TILES):
            quantize_w1(t)
            make_h(t, [(0, QUARTER), (QUARTER, QUARTER)])
            make_h(t, [(HALF, HALF)])
        put(0, idx2, HALF, HALF, h_sb[0][:, HALF:], wgs_sb)

        w2_grouped = tile([P, H * PACK], BF16, "w2_grouped")
        w2_codes = tile([P, H], U32, "w2_codes")
        w2_plane = tile([P, H], U8, "w2_plane")
        nc.scalar.activation(
            out=w2_grouped[:].rearrange("p (c i) -> p c i", i=PACK), in_=w2_raw[:].rearrange("p i c -> p c i"), func=ACT.Copy
        )
        quantize(w2_codes[:], w2_plane[:], w2_grouped[:])

        for t in range(TILES):
            nc.scalar.activation(out=neg_base[t][:], in_=neg_base[t][:], func=ACT.Copy, scale=-1.0)

        x0 = []
        d_t0 = tile([P, PACK * HALF], BF16, "d_t0", tag="d_t")
        last = TILES - 1
        for t in range(1, TILES):
            put(t, idx2, 0, S, h_sb[t][:], wgs_sb)
            for done in [t - 1, t] if t == last - 1 else [t - 1] if t < last else []:
                x0.append(tile([P, HALF], F32, f"x0_{done}", tag=f"h_then_x{t}" if done < t else None))
                pick(done, 0, HALF, x0[done][:])
                departure_t(turn[(done + 1) % 2], d_t0, done, 0, HALF, x0[done])
        x0.append(tile([P, HALF], F32, f"x0_{last}"))
        for quarter in range(2):
            cols = slice(quarter * QUARTER, (quarter + 1) * QUARTER)
            pick(last, quarter * QUARTER, QUARTER, x0[last][:, cols])
            departure_t(turn[quarter], d_t0, last, quarter * QUARTER, QUARTER, x0[last][:, cols])

        x1_early = tile([P, last, HALF], F32, "x1_early", tag="wgs_then_x")
        for t in range(last):
            pick(t, HALF, HALF, x1_early[:, t, :])

        d_codes = [tile([P, HALF], U32, f"d_codes{h}") for h in range(2)]
        d_plane = [tile([P, HALF], U8, f"d_plane{h}") for h in range(2)]
        z_codes = [tile([P, HALF], U32, f"z_codes{h}") for h in range(2)]
        z_plane = [tile([P, HALF], U8, f"z_plane{h}") for h in range(2)]
        for quarter in range(2):
            cols = slice(quarter * QUARTER, (quarter + 1) * QUARTER)
            d_q = tile([P, PACK * QUARTER], BF16, f"d_q{quarter}")
            z_q = tile([P, PACK * QUARTER], BF16, f"z_q{quarter}", tag=f"z_then_x{quarter}")
            group_d_z(d_t0, quarter, d_q[:], z_q[:])
            quantize(d_codes[0][:, cols], d_plane[0][:, cols], d_q[:])
            quantize(z_codes[0][:, cols], z_plane[0][:, cols], z_q[:])

        x1_last = tile([P, HALF], F32, "x1_last", tag="z_then_x0")
        pick(last, HALF, HALF, x1_last[:])
        x1 = [x1_early[:, t, :] for t in range(last)] + [x1_last[:]]

        def score(t, first, count):
            half = first // HALF
            cols = slice(first % HALF, first % HALF + count)
            acc = bank(f"e_acc{t}_{first}", "acc", 6)[:, :count]
            nc.tensor.matmul_mx(
                out=acc,
                lhsT=w2_codes[:, t * P : (t + 1) * P].bitcast(FP8X4),
                lhsT_scale=w2_plane[:, t * P : (t + 1) * P],
                rhs=d_codes[half][:, cols].bitcast(FP8X4),
                rhs_scale=d_plane[half][:, cols],
                start=True,
                stop=False,
            )
            nc.tensor.matmul_mx(
                out=acc,
                lhsT=w4_codes[:, 2 * t * P : 2 * (t + 1) * P].bitcast(FP4X4),
                lhsT_scale=w4_plane[:, t * P : (t + 1) * P],
                rhs=z_codes[half][:, cols].bitcast(FP8X4),
                rhs_scale=z_plane[half][:, cols],
                start=False,
                stop=True,
            )
            return acc

        def larger(t, acc, x, y):
            nc.vector.scalar_tensor_tensor(out=y, in0=acc, scalar=b2_sb[:, t, 0:1], in1=x, op0=ALU.add, op1=ALU.max)

        pieces = [(0, 0, QUARTER), (0, QUARTER, QUARTER), (1, 0, HALF)]
        y0 = []
        for t, first, count in pieces:
            y = tile([P, count], F32, f"y0_{t}_{first}", tag="z_then_x1" if (t, first) == (0, 0) else None)
            larger(t, score(t, first, count), x0[t][:, first : first + count], y[:])
            y0.append(y)
        for (t, first, count), y in zip(pieces, y0):
            put(t, idx4, first, count, y[:], wgo_sb)

        d_t1 = tile([P, PACK * HALF], BF16, "d_t1", tag="d_t")
        for t in range(TILES):
            departure_t(turn[t % 2], d_t1, t, HALF, HALF, x1[t])
        held = range(2, TILES)
        acc0_held = {t: score(t, 0, HALF) for t in held}
        d_h = tile([P, PACK * HALF], BF16, "d_h")
        z_h = tile([P, PACK * HALF], BF16, "z_h", tag="z_then_y")
        for quarter in range(2, 4):
            cols = slice((quarter - 2) * PACK * QUARTER, (quarter - 1) * PACK * QUARTER)
            group_d_z(d_t1, quarter, d_h[:, cols], z_h[:, cols])
        quantize(d_codes[1][:], d_plane[1][:], d_h[:])
        quantize(z_codes[1][:], z_plane[1][:], z_h[:])

        y0_held = tile([P, len(held) * HALF], F32, "y0_held", tag="z_then_y")
        for i, t in enumerate(held):
            larger(t, acc0_held[t], x0[t][:], y0_held[:, i * HALF : (i + 1) * HALF])
        acc1 = [score(t, HALF, HALF) for t in range(TILES)]
        for i, t in enumerate(held):
            put(t, idx4, 0, HALF, y0_held[:, i * HALF : (i + 1) * HALF], wgo_sb)
        y1 = [tile([P, HALF], F32, f"y1_{t}") for t in range(TILES)]
        for t in range(TILES):
            larger(t, acc1[t], x1[t], y1[t][:])
        for t in range(TILES):
            put(t, idx4, HALF, HALF, y1[t][:], wgo_sb)
            nc.sync.dma_start(out=out[t * P : (t + 1) * P, :], in_=page[t][:])
